import numpy as np
import ml_dtypes


def mxq(x, axis, fmt="e4m3"):
    dtype, down = {"e4m3": (ml_dtypes.float8_e4m3fn, 7), "e5m2": (ml_dtypes.float8_e5m2, 14)}[fmt]
    v = np.moveaxis(np.asarray(x, np.float32).astype(ml_dtypes.bfloat16).astype(np.float64), axis, -1)
    blocks = v.reshape(v.shape[:-1] + (-1, 32))
    amax = np.abs(blocks).max(-1, keepdims=True)
    byte = np.maximum(np.where(amax > 0, np.frexp(amax)[1] - 1 + 127, 0) - down, 1)
    scale = np.exp2(byte - 127.0)
    codes = (blocks / scale).astype(np.float32).astype(dtype).astype(np.float64)
    return np.moveaxis((codes * scale).reshape(v.shape), -1, axis)


WIDE = False


def mx_kscale(k):
    if not WIDE:
        return np.ones(k)
    levels = np.array([10, -10, 5, -5, 0])
    if k % 512:
        return np.exp2(np.random.permutation(np.resize(levels, k // 32))).repeat(32)
    a = np.empty((k // 512, 16))
    for p in range(k // 512):
        a[p, :8] = np.random.permutation(np.resize(levels, 8))
        for g in range(8):
            far = levels[np.abs(levels - a[p, g]) >= 10]
            a[p, g + 8] = far[np.random.randint(len(far))]
    return np.exp2(a.ravel()).repeat(32)


BF16 = ml_dtypes.bfloat16


def bf(x):
    return np.asarray(x, np.float32).astype(BF16)


def f64(x):
    return np.asarray(x).astype(np.float64)


E2M1 = np.array([0.0, 0.5, 1.0, 1.5, 2.0, 3.0, 4.0, 6.0, -0.0, -0.5, -1.0, -1.5, -2.0, -3.0, -4.0, -6.0])


def pack_weight(w, fmt):
    k, n = w.shape
    w = f64(bf(w)).reshape(k // 32, 32, n)
    amax = np.abs(w).max(1)
    if fmt == "e4m3":
        byte = np.frexp(amax)[1] - 1 + 127 - 7
    else:
        mant, ex = np.frexp(amax / 6.0)
        byte = np.where(mant > 0.5, ex, ex - 1) + 127
    byte = np.clip(np.where(amax > 0, byte, 1), 1, 254)
    scaled = (w * np.exp2(127.0 - byte)[:, None, :]).reshape(k, n).astype(np.float32)
    by_word = np.ascontiguousarray(scaled.reshape(k // 512, 128, 4, n).transpose(0, 1, 3, 2))
    if fmt == "e4m3":
        words = by_word.astype(ml_dtypes.float8_e4m3fn).view(np.uint8)
    else:
        c = by_word.astype(ml_dtypes.float4_e2m1fn).view(np.uint8) & 0xF
        words = c[..., 0::2] | (c[..., 1::2] << 4)
    return np.ascontiguousarray(words), np.ascontiguousarray(byte.astype(np.uint8).reshape(k // 512, 16, n))


def unpack_weight(words, scales, fmt):
    g, p, n, _ = words.shape
    if fmt == "e4m3":
        vals = np.ascontiguousarray(words).view(ml_dtypes.float8_e4m3fn).astype(np.float64)
    else:
        nib = np.empty((g, p, n, 4), np.uint8)
        nib[..., 0::2] = words & 0xF
        nib[..., 1::2] = words >> 4
        vals = E2M1[nib]
    vals = vals * np.repeat(np.exp2(scales.astype(np.float64) - 127.0), 8, axis=1)[..., None]
    return vals.transpose(0, 1, 3, 2).reshape(g * 512, n)
def pack4(w):
    words, scales = pack_weight(w, "e2m1")
    return words.reshape(words.shape[0], 128, -1), scales


def unpack4(words, scales):
    return unpack_weight(words.reshape(words.shape[0], 128, -1, 2), scales, "e2m1")


def planes(Y):
    n, m = Y.shape
    b = f64(bf(Y)).reshape(n // 32, 32, m)
    amax = np.abs(b).max(1)
    byte = np.clip(np.where(amax > 0, np.frexp(amax)[1] - 1 + 127 - 7, 1), 1, 254)
    codes = (b * np.exp2(127.0 - byte)[:, None, :]).reshape(n, m).astype(np.float32).astype(ml_dtypes.float8_e4m3fn).view(np.uint8)
    words = codes.reshape(n // 512, 128, 4, m).transpose(0, 1, 3, 2)
    return np.ascontiguousarray(words), np.ascontiguousarray(byte.astype(np.uint8).reshape(n // 512, 16, m))


N, D, K, O = 1024, 1024, 1024, 1024


def setup_inputs():
    p, t = mx_kscale(D), mx_kscale(K)
    z = bf(np.random.standard_normal((N, D)) * p)
    a1_words, a1_scales = pack4(np.random.standard_normal((D, K)) / np.sqrt(D) / p[:, None] * t)
    g1 = bf(1.0 + 0.1 * np.random.standard_normal(K))
    s_words, s_scales = pack4(np.random.standard_normal((K, O)) / np.sqrt(K) / t[:, None])
    c = bf(0.5 * np.random.standard_normal(O))
    a2_words, a2_scales = pack4(np.random.standard_normal((D, O)) / np.sqrt(D) / p[:, None])
    return {"z": z,
            "a1_words": a1_words,
            "a1_scales": a1_scales,
            "g1": g1,
            "s_words": s_words,
            "s_scales": s_scales,
            "c": c,
            "a2_words": a2_words,
            "a2_scales": a2_scales}


def core(z, a1_words, a1_scales, g1, s_words, s_scales, c, a2_words, a2_scales):
    zq = mxq(f64(z), 1, "e4m3")
    u1 = zq @ unpack4(a1_words, a1_scales)
    x1 = u1 * f64(g1)[None, :]
    v = mxq(x1, 1, "e4m3") @ unpack4(s_words, s_scales)
    v = v + f64(c)[None, :]
    u2 = zq @ unpack4(a2_words, a2_scales)
    return u2 * v


def reference(z, a1_words, a1_scales, g1, s_words, s_scales, c, a2_words, a2_scales):
    R_out = core(z, a1_words, a1_scales, g1, s_words, s_scales, c, a2_words, a2_scales)
    words, scales = planes(R_out.T)
    return R_out, words, scales

@@ -1,0 +1,294 @@
+from contextlib import ExitStack
+
+import concourse.mybir as mybir
+
+F32 = mybir.dt.float32
+BF16 = mybir.dt.bfloat16
+I32 = mybir.dt.int32
+U32 = mybir.dt.uint32
+U8 = mybir.dt.uint8
+E4M3X4 = mybir.dt.float8_e4m3fn_x4
+E2M1X4 = mybir.dt.float4_e2m1fn_x4
+ALU = mybir.AluOpType
+
+P = 128
+SIZE = 1024
+HALF = 512
+TILES = SIZE // P
+FLOPS = 3 * 2 * SIZE * SIZE * SIZE
+
+
+def tile_pinetnestedcoupledcpdegreetwo_x2_kernel(
+    tc, z, a1_words, a1_scales, g1, s_words, s_scales, c, a2_words, a2_scales, out_0, out_1, out_2
+):
+    nc = tc.nc
+    out_words = out_1.rearrange("g p m b -> p g (m b)")
+
+    with ExitStack() as ctx:
+        keep = ctx.enter_context(tc.tile_pool(name="keep", bufs=1))
+        work = ctx.enter_context(tc.tile_pool(name="work", bufs=3))
+        psum = ctx.enter_context(tc.psum_pool(name="psum", bufs=4))
+        ctx.enter_context(tc.manual_schedule())
+
+        gc_rows = keep.tile([P, P], BF16, name="gc_rows", align_bytes=64)
+        nc.vector.memset(gc_rows[:], 0.0)
+        planes = {}
+        words = {}
+        for name in ("a1", "a2", "s"):
+            words[name] = keep.tile([P, 2, 2 * SIZE], U8, name=name + "_w", align_bytes=64)
+            planes[name] = keep.tile([P, 2, SIZE], U8, name=name + "_sc", align_bytes=64)
+        nc.vector.memset(planes["a1"][:].rearrange("p g n -> p (g n)").bitcast(I32), 0)
+        diff = keep.tile([P, P], I32, name="diff", align_bytes=64)
+        nc.gpsimd.iota(diff[:], pattern=[[-1, P]], base=0, channel_multiplier=1)
+        nc.scalar.dma_start(out=gc_rows[0:8, :], in_=g1.rearrange("(r n) -> r n", n=P))
+        nc.scalar.dma_start(out=gc_rows[8:16, :], in_=c.rearrange("(r n) -> r n", n=P))
+        ident = keep.tile([P, P], F32, name="ident", align_bytes=64)
+        ident_bf = keep.tile([P, P], BF16, name="ident_bf", align_bytes=64)
+        nc.vector.tensor_single_scalar(out=ident[:], in_=diff[:], scalar=0, op=ALU.is_equal)
+        nc.vector.tensor_single_scalar(out=ident_bf[:], in_=diff[:], scalar=0, op=ALU.is_equal)
+        nc.vector.memset(planes["a2"][:].rearrange("p g n -> p (g n)").bitcast(I32), 0)
+        nc.vector.memset(planes["s"][:].rearrange("p g n -> p (g n)").bitcast(I32), 0)
+
+        z_sb = []
+        for t in range(TILES):
+            z_sb.append(keep.tile([P, SIZE], BF16, name="z_sb" + str(t), align_bytes=64))
+
+        def load_z(t):
+            nc.sync.dma_start(out=z_sb[t][:], in_=z[t * P : (t + 1) * P, :])
+
+        def load_words(name, src, lo, hi):
+            nc.sync.dma_start(
+                out=words[name][:, :, lo:hi].bitcast(I32),
+                in_=src.rearrange("g p b -> p g b")[:, :, lo:hi].bitcast(I32),
+            )
+
+        def load_scales(name, src, queue):
+            for q in range(4):
+                queue.dma_start(
+                    out=planes[name][32 * q : 32 * q + 4, :, :].bitcast(I32),
+                    in_=src[:, 4 * q : 4 * q + 4, :].rearrange("g q n -> q g n").bitcast(I32),
+                )
+
+        load_z(0)
+        load_scales("a1", a1_scales, nc.scalar)
+        load_words("a1", a1_words, 0, SIZE)
+        load_words("a1", a1_words, SIZE, 2 * SIZE)
+        load_z(1)
+        load_scales("a2", a2_scales, nc.sync)
+        load_words("a2", a2_words, 0, 2 * SIZE)
+        load_z(2)
+        load_scales("s", s_scales, nc.sync)
+        load_words("s", s_words, 0, 2 * SIZE)
+        for t in range(3, TILES):
+            load_z(t)
+
+        oc = keep.tile([P, 2, SIZE], U32, name="oc", align_bytes=64)
+        osc = keep.tile([P, 2, SIZE], U8, name="osc", align_bytes=64)
+        live = {}
+
+        def z_turn(t):
+            turned = psum.tile([P, 2, 2, P], F32, name="zt", tag="mm")
+            zw = z_sb[t][:].bitcast(F32)
+            for g in range(2):
+                for u in range(2):
+                    nc.tensor.transpose(turned[:, g, u, :], zw[:, 256 * g + u : 256 * (g + 1) : 2], ident[:])
+            live["zt", t] = turned
+
+        def word_copy(key, tag, t):
+            turned = live[key, t]
+            grouped = work.tile([P, 2 * P * 4], BF16, name=tag, tag=tag, align_bytes=64)
+            nc.scalar.copy(
+                out=grouped[:].bitcast(F32).rearrange("p (g n u) -> p g n u", g=2, u=2),
+                in_=turned[:].rearrange("p g u n -> p g n u"),
+            )
+            live[tag, t] = grouped
+
+        def quant(tag, t, codes_name):
+            codes = keep.tile([P, 2 * P], U32, name=codes_name + str(t), align_bytes=64)
+            scales = keep.tile([P, 2 * P], U8, name=codes_name + "s" + str(t), align_bytes=64)
+            nc.vector.quantize_mx(out=codes[:].bitcast(E4M3X4), scales=scales[:], in_=live[tag, t][:])
+            live[codes_name, t] = (codes, scales)
+
+        def product(codes_name, t, name, h, bank):
+            codes, scales = live[codes_name, t]
+            for g in range(2):
+                nc.tensor.matmul_mx(
+                    out=bank[:],
+                    lhsT=codes[:, g * P : (g + 1) * P].bitcast(E4M3X4),
+                    lhsT_scale=scales[:, g * P : (g + 1) * P],
+                    rhs=words[name][:, g, h * SIZE : (h + 1) * SIZE].bitcast(E2M1X4),
+                    rhs_scale=planes[name][:, g, h * HALF : (h + 1) * HALF],
+                    start=(g == 0),
+                    stop=(g == 1),
+                )
+
+        def u1(t):
+            for h in range(2):
+                bank = psum.tile([P, HALF], F32, name="u1", tag="mm")
+                product("zq", t, "a1", h, bank)
+                live["u1", t, h] = bank
+
+        def u2(t):
+            for h in range(2):
+                bank = psum.tile([P, HALF], F32, name="u2", tag="u2", bufs=2)
+                product("zq", t, "a2", h, bank)
+                live["u2", t, h] = bank
+
+        def v(t, h):
+            bank = psum.tile([P, HALF], F32, name="v", tag="v", bufs=2)
+            product("xq", t, "s", h, bank)
+            live["v", t, h] = bank
+
+        def gain(t, h):
+            if h == 0:
+                x1 = work.tile([P, 2, HALF], BF16, name="x1", tag="x1", align_bytes=64)
+                live["x1", t] = x1
+            nc.vector.tensor_tensor(
+                out=live["x1", t][:, h, :].rearrange("p (u i e) -> p u i e", u=2, e=2),
+                in0=live["u1", t, h][:].rearrange("p (i u e) -> p u i e", u=2, e=2),
+                in1=g_bc[:, h * HALF : (h + 1) * HALF].rearrange("p (i u e) -> p u i e", u=2, e=2),
+                op=ALU.mult,
+            )
+
+        def turn(src, t, key):
+            turned = psum.tile([P, 2, 2, P], F32, name=key, tag="mm")
+            for g in range(2):
+                half_words = live[src, t][:, g, :].bitcast(F32)
+                for u in range(2):
+                    nc.tensor.transpose(turned[:, g, u, :], half_words[:, u * P : (u + 1) * P], ident[:])
+            live[key, t] = turned
+
+        def add(t, h):
+            if h == 0:
+                live["vc", t] = work.tile([P, 2, HALF], F32, name="vc", tag="vc", align_bytes=64)
+                live["o", t] = work.tile([P, 2, HALF], F32, name="o", tag="o", align_bytes=64)
+            nc.vector.tensor_tensor(
+                out=live["vc", t][:, h, :], in0=live["v", t, h][:], in1=c_bc[:, h * HALF : (h + 1) * HALF], op=ALU.add
+            )
+
+        def mul(t, h):
+            nc.vector.tensor_tensor(
+                out=live["o", t][:, h, :], in0=live["u2", t, h][:], in1=live["vc", t][:, h, :], op=ALU.mult
+            )
+
+        def store_rows(t, h):
+            rows = out_0[t * P : (t + 1) * P, :]
+            if h is None:
+                nc.sync.dma_start(out=rows, in_=live["o", t][:].rearrange("p h n -> p (h n)"))
+            else:
+                nc.sync.dma_start(out=rows[:, h * HALF : (h + 1) * HALF], in_=live["o", t][:, h, :])
+
+        def cast(t, h):
+            if h == 0:
+                live["ob", t] = work.tile([P, 2, HALF], BF16, name="ob", tag="ob", align_bytes=64)
+            nc.scalar.copy(
+                out=live["ob", t][:, h, :].rearrange("p (u i e) -> p u i e", u=2, e=2),
+                in_=live["o", t][:, h, :].rearrange("p (i u e) -> p u i e", u=2, e=2),
+            )
+
+        def out_quant(t):
+            for g in range(2):
+                nc.vector.quantize_mx(
+                    out=oc[:, g, t * P : (t + 1) * P].bitcast(E4M3X4),
+                    scales=osc[:, g, t * P : (t + 1) * P],
+                    in_=live["oi", t][:, g * HALF : (g + 1) * HALF],
+                )
+
+        def store_words(t0, t1):
+            nc.sync.dma_start(
+                out=out_words[:, :, t0 * HALF : t1 * HALF].bitcast(I32), in_=oc[:, :, t0 * P : t1 * P].bitcast(I32)
+            )
+
+        def store_scales(t0, t1):
+            for q in range(4):
+                nc.sync.dma_start(
+                    out=out_2[:, 4 * q : 4 * q + 4, t0 * P : t1 * P].rearrange("g q m -> q g m").bitcast(I32),
+                    in_=osc[32 * q : 32 * q + 4, :, t0 * P : t1 * P].bitcast(I32),
+                )
+
+        z_turn(0)
+        word_copy("zt", "zi", 0)
+        quant("zi", 0, "zq")
+        gc_turned = psum.tile([P, P], BF16, name="gct", tag="mm")
+        nc.tensor.transpose(gc_turned[:], gc_rows[:], ident_bf[:])
+        gc_cols = keep.tile([P, 16], BF16, name="gc_cols", align_bytes=64)
+        nc.vector.tensor_copy(out=gc_cols[:], in_=gc_turned[:, 0:16])
+        g_bc = keep.tile([P, SIZE], BF16, name="g_bc", align_bytes=64)
+        c_bc = keep.tile([P, SIZE], BF16, name="c_bc", align_bytes=64)
+
+        def spread(dst, first):
+            bank = psum.tile([P, SIZE], BF16, name="bc", tag="mm")
+            for m in range(8):
+                nc.tensor.transpose(
+                    bank[:, m * P : (m + 1) * P],
+                    gc_cols[:, first + m : first + m + 1].to_broadcast([P, P]),
+                    ident_bf[:],
+                )
+            nc.scalar.copy(out=dst[:], in_=bank[:])
+
+        spread(g_bc, 0)
+        u1(0)
+        gain(0, 0)
+        gain(0, 1)
+        z_turn(1)
+        word_copy("zt", "zi", 1)
+        quant("zi", 1, "zq")
+        spread(c_bc, 8)
+        turn("x1", 0, "xt")
+        z_turn(2)
+
+        for k in range(TILES):
+            word_copy("xt", "xi", k)
+            if k >= 2:
+                word_copy("ot", "oi", k - 2)
+            if k + 2 < TILES:
+                word_copy("zt", "zi", k + 2)
+            quant("xi", k, "xq")
+            if k + 1 < TILES:
+                u1(k + 1)
+            u2(k)
+            if k + 1 < TILES:
+                gain(k + 1, 0)
+            if k + 2 < TILES:
+                quant("zi", k + 2, "zq")
+            if k + 1 < TILES:
+                gain(k + 1, 1)
+            if k >= 2:
+                out_quant(k - 2)
+                if k % 2 == 1:
+                    store_words(k - 3, k - 1)
+                if k == 5:
+                    store_scales(0, 4)
+            v(k, 0)
+            v(k, 1)
+            if k >= 1:
+                cast(k - 1, 0)
+                cast(k - 1, 1)
+            last = k == TILES - 1
+            add(k, 0)
+            if last:
+                mul(k, 0)
+                store_rows(k, 0)
+                add(k, 1)
+            else:
+                add(k, 1)
+                mul(k, 0)
+            mul(k, 1)
+            store_rows(k, 1 if last else None)
+            if k + 1 < TILES:
+                turn("x1", k + 1, "xt")
+            if k >= 1:
+                turn("ob", k - 1, "ot")
+            if k + 3 < TILES:
+                z_turn(k + 3)
+
+        word_copy("ot", "oi", 6)
+        out_quant(6)
+        store_words(6, 7)
+        cast(7, 0)
+        cast(7, 1)
+        turn("ob", 7, "ot")
+        word_copy("ot", "oi", 7)
+        out_quant(7)
+        store_words(7, 8)
+        store_scales(4, 8)

@@ -10,12 +10,37 @@ U8 = mybir.dt.uint8
 E4M3X4 = mybir.dt.float8_e4m3fn_x4
 E2M1X4 = mybir.dt.float4_e2m1fn_x4
 ALU = mybir.AluOpType
+ACT = mybir.ActivationFunctionType
 
 P = 128
 SIZE = 1024
 HALF = 512
+PAIR = 2 * P
 TILES = SIZE // P
+LOWER = 4
 FLOPS = 3 * 2 * SIZE * SIZE * SIZE
+
+ORDER = (
+    "perm0 zturn0 biasturn0 zgroup0 zturn1 perm1 zgroup1 biasspread0 perm2 zquant0 perm3 zturn2 gains0",
+    "u1A0 zquant1 zgroup2 gainA0 zorder3 u1B0 zorder4 u1A1 u1B1 gainB0 zorder5",
+    "zturn3 zorder6 gainA1 zturn4 zturn5 xquant0 zturn6 zquant2 zorder7 zgroup3 zquant3 zturn7 gainB1",
+    "u1A2 u1B2 gainA2 zgroup4 u1A3 zgroup5 zpairA4 zpairB4 zgroup6 u1B3 zgroup7 zpairA6 zpairB6 gainB2",
+    "scaleA3 xquant1",
+    "vA0 xquant2 u2A0 scaleB3 mixA3 u1wide0 u1wide1 addA0 vB0 mulA0 addB0 vA1 mixL0 u2B0 mixR0 vB1 addA1",
+    "mixB3",
+    "u2A1 u1wide2 vA2 addB1 u1wide3 mulB0 rows0 u2B1 mixR1 mixL1 mulA1 u2A2 vB2 addA2 xwide0 castA0",
+    "xquant3 mulB1 rows1",
+    "vA3 mulA2 addB2 castB0 addA3 u2B2 mulB2 rows2 vB3 castA1 u2A3 u2B3 addB3 u2A4 xwide1",
+    "vA4 vB4 oturn0 castB1 oturn1 mulA3 mulB3 rows3 castA2 castB2",
+    "vA5 addA4 u2B4 castA3 u2A5 ogroup0 addB4 mulA4 castB3 vB5 addA5 ogroup1 u2B5 mulB4 rows4 castA4",
+    "mulA5",
+    "vA6 addB5 oturn2 opairB0 opairA0 wordpair0 addA6 mulB5 rows5 vB6 ogroup2 castB4",
+    "vA7 u2A6 oturn3 vB7 u2B6 castA5 oturn4 castB5 ogroup3 u2A7 addB6 u2B7 addA7 mulA6 addB7 mulB6 rows6",
+    "castA6 ogroup4 castB6 opairA2 opairB2 scales0 wordpair2 oturn5 mulA7 rowsA7 lastA7 oturn6 ogroup5",
+    "lastB7 opairB4 opairA4 wordpair4",
+    "oturnA7 ogroup6 ooneA6 ogroupA7 oturnB7 ooneB6 wordone6 ooneA7 ogroupB7 ooneB7 wordone7 scales1",
+    "mulB7 rowsB7",
+)
 
 
 def tile_pinetnestedcoupledcpdegreetwo_x2_kernel(
@@ -26,41 +51,60 @@ def tile_pinetnestedcoupledcpdegreetwo_x2_kernel(
 
     with ExitStack() as ctx:
         keep = ctx.enter_context(tc.tile_pool(name="keep", bufs=1))
-        work = ctx.enter_context(tc.tile_pool(name="work", bufs=3))
-        psum = ctx.enter_context(tc.psum_pool(name="psum", bufs=4))
+        work = ctx.enter_context(tc.tile_pool(name="work", bufs=5))
+        psum = ctx.enter_context(tc.psum_pool(name="psum", bufs=8))
         ctx.enter_context(tc.manual_schedule())
+        live = {}
 
-        gc_rows = keep.tile([P, P], BF16, name="gc_rows", align_bytes=64)
-        nc.vector.memset(gc_rows[:], 0.0)
-        planes = {}
+        c_rows = keep.tile([P, P], BF16, name="c_rows", align_bytes=64)
+        nc.vector.memset(c_rows[:], 0.0)
         words = {}
+        planes = {}
+        for name in ("a2", "s"):
+            words[name] = keep.tile([P, 2, 2 * SIZE], U8, name=name + "_words_sb", align_bytes=64)
         for name in ("a1", "a2", "s"):
-            words[name] = keep.tile([P, 2, 2 * SIZE], U8, name=name + "_w", align_bytes=64)
-            planes[name] = keep.tile([P, 2, SIZE], U8, name=name + "_sc", align_bytes=64)
-        nc.vector.memset(planes["a1"][:].rearrange("p g n -> p (g n)").bitcast(I32), 0)
+            planes[name] = keep.tile([P, 2, SIZE], U8, name=name + "_plane", align_bytes=64)
+
+        def clear(name):
+            nc.vector.memset(planes[name][:].rearrange("p g n -> p (g n)").bitcast(I32), 0)
+
+        clear("a1")
         diff = keep.tile([P, P], I32, name="diff", align_bytes=64)
         nc.gpsimd.iota(diff[:], pattern=[[-1, P]], base=0, channel_multiplier=1)
-        nc.scalar.dma_start(out=gc_rows[0:8, :], in_=g1.rearrange("(r n) -> r n", n=P))
-        nc.scalar.dma_start(out=gc_rows[8:16, :], in_=c.rearrange("(r n) -> r n", n=P))
         ident = keep.tile([P, P], F32, name="ident", align_bytes=64)
         ident_bf = keep.tile([P, P], BF16, name="ident_bf", align_bytes=64)
         nc.vector.tensor_single_scalar(out=ident[:], in_=diff[:], scalar=0, op=ALU.is_equal)
         nc.vector.tensor_single_scalar(out=ident_bf[:], in_=diff[:], scalar=0, op=ALU.is_equal)
-        nc.vector.memset(planes["a2"][:].rearrange("p g n -> p (g n)").bitcast(I32), 0)
-        nc.vector.memset(planes["s"][:].rearrange("p g n -> p (g n)").bitcast(I32), 0)
+        clear("a2")
+        clear("s")
 
-        z_sb = []
-        for t in range(TILES):
-            z_sb.append(keep.tile([P, SIZE], BF16, name="z_sb" + str(t), align_bytes=64))
+        z_sb = [keep.tile([P, SIZE], BF16, name="z_sb" + str(t), align_bytes=64) for t in range(TILES)]
+        a1_raw = [keep.tile([P, 2, SIZE], U8, name="a1_raw" + str(b), align_bytes=64) for b in range(2)]
+        a1_cols = keep.tile([P, 2, 2 * SIZE], U8, name="a1_cols", align_bytes=64)
+        a1_plane = keep.tile([P, 2, SIZE], U8, name="a1_plane_cols", align_bytes=64)
+        g_raw = keep.tile([P, 2, 4], BF16, name="g_raw", align_bytes=64)
+        g_cols = keep.tile([P, 2, 4], F32, name="g_cols", align_bytes=64)
+        c_cols = keep.tile([P, 8], BF16, name="c_cols", align_bytes=64)
+        c_all = keep.tile([P, SIZE], BF16, name="c_all", align_bytes=64)
+        zq_upper = keep.tile([P, 2, HALF], U32, name="zq_upper", align_bytes=64)
+        zs_upper = keep.tile([P, 2, HALF], U8, name="zs_upper", align_bytes=64)
+        xq_upper = keep.tile([P, 2, HALF], U32, name="xq_upper", align_bytes=64)
+        xs_upper = keep.tile([P, 2, HALF], U8, name="xs_upper", align_bytes=64)
+        oq_pair = [keep.tile([P, 2, PAIR], U32, name="oq_pair" + str(i), align_bytes=64) for i in range(3)]
+        oq_one = [keep.tile([P, 2, P], U32, name="oq_one" + str(i), align_bytes=64) for i in range(2)]
+        os_half = [keep.tile([P, 2, HALF], U8, name="os_half" + str(i), align_bytes=64) for i in range(2)]
 
         def load_z(t):
             nc.sync.dma_start(out=z_sb[t][:], in_=z[t * P : (t + 1) * P, :])
 
-        def load_words(name, src, lo, hi):
+        def load_a1(b):
             nc.sync.dma_start(
-                out=words[name][:, :, lo:hi].bitcast(I32),
-                in_=src.rearrange("g p b -> p g b")[:, :, lo:hi].bitcast(I32),
+                out=a1_raw[b][:].bitcast(I32),
+                in_=a1_words.rearrange("g p b -> p g b")[:, :, b * SIZE : (b + 1) * SIZE].bitcast(I32),
             )
+
+        def load_words(name, src):
+            nc.sync.dma_start(out=words[name][:].bitcast(I32), in_=src.rearrange("g p b -> p g b").bitcast(I32))
 
         def load_scales(name, src, queue):
             for q in range(4):
@@ -69,226 +113,353 @@ def tile_pinetnestedcoupledcpdegreetwo_x2_kernel(
                     in_=src[:, 4 * q : 4 * q + 4, :].rearrange("g q n -> q g n").bitcast(I32),
                 )
 
-        load_z(0)
+        load_a1(0)
         load_scales("a1", a1_scales, nc.scalar)
-        load_words("a1", a1_words, 0, SIZE)
-        load_words("a1", a1_words, SIZE, 2 * SIZE)
+        load_z(0)
+        load_a1(1)
+        nc.gpsimd.dma_start(out=c_rows[0:8, :], in_=c.rearrange("(r n) -> r n", n=P))
+        nc.gpsimd.dma_start(out=g_raw[:], in_=g1.rearrange("(g p t) -> p g t", p=P, t=4))
         load_z(1)
-        load_scales("a2", a2_scales, nc.sync)
-        load_words("a2", a2_words, 0, 2 * SIZE)
-        load_z(2)
         load_scales("s", s_scales, nc.sync)
-        load_words("s", s_words, 0, 2 * SIZE)
+        load_words("s", s_words)
+        load_z(2)
+        load_scales("a2", a2_scales, nc.sync)
+        load_words("a2", a2_words)
         for t in range(3, TILES):
             load_z(t)
 
-        oc = keep.tile([P, 2, SIZE], U32, name="oc", align_bytes=64)
-        osc = keep.tile([P, 2, SIZE], U8, name="osc", align_bytes=64)
-        live = {}
+        def bias_turn():
+            turned = psum.tile([P, P], BF16, name="c_turned", tag="bank")
+            nc.tensor.transpose(turned[:], c_rows[:], ident_bf[:])
+            nc.scalar.copy(out=c_cols[:], in_=turned[:, 0:8])
+
+        def bias_spread():
+            bank = psum.tile([P, SIZE], BF16, name="c_spread", tag="bank")
+            for m in range(8):
+                nc.tensor.transpose(
+                    bank[:, m * P : (m + 1) * P], c_cols[:, m : m + 1].to_broadcast([P, P]), ident_bf[:]
+                )
+            nc.scalar.copy(out=c_all[:], in_=bank[:])
+
+        def gains():
+            nc.vector.tensor_copy(
+                out=g_cols[:].rearrange("p g t -> p (g t)"), in_=g_raw[:].rearrange("p g t -> p (g t)")
+            )
+
+        def permute(b, g):
+            nc.vector.tensor_copy(
+                out=a1_cols[:, g, b * SIZE : (b + 1) * SIZE].rearrange("p (t m c) -> p t m c", t=4, c=2),
+                in_=a1_raw[b][:, g, :].rearrange("p (m t c) -> p t m c", t=4, c=2),
+            )
+            nc.vector.tensor_copy(
+                out=a1_plane[:, g, b * HALF : (b + 1) * HALF].rearrange("p (t m) -> p t m", t=4),
+                in_=planes["a1"][:, g, b * HALF : (b + 1) * HALF].rearrange("p (m t) -> p t m", t=4),
+            )
+
+        def z_order(t):
+            ordered = work.tile([P, 2, 2, P], F32, name="z_words", tag="z_words", align_bytes=64)
+            nc.scalar.copy(
+                out=ordered[:], in_=z_sb[t][:].bitcast(F32).rearrange("p (g w u) -> p g u w", g=2, u=2)
+            )
+            live["z words", t] = ordered
 
         def z_turn(t):
-            turned = psum.tile([P, 2, 2, P], F32, name="zt", tag="mm")
-            zw = z_sb[t][:].bitcast(F32)
+            turned = psum.tile([P, 2, 2, P], F32, name="z_turned", tag="bank")
             for g in range(2):
                 for u in range(2):
-                    nc.tensor.transpose(turned[:, g, u, :], zw[:, 256 * g + u : 256 * (g + 1) : 2], ident[:])
-            live["zt", t] = turned
+                    if t < 3:
+                        source = z_sb[t][:].bitcast(F32)[:, 256 * g + u : 256 * (g + 1) : 2]
+                    else:
+                        source = live["z words", t][:, g, u, :]
+                    nc.tensor.transpose(turned[:, g, u, :], source, ident[:])
+            live["z turned", t] = turned
 
-        def word_copy(key, tag, t):
-            turned = live[key, t]
-            grouped = work.tile([P, 2 * P * 4], BF16, name=tag, tag=tag, align_bytes=64)
+        def group_pair(kind, t, bufs):
+            pair, at = t // 2, (t % 2) * P
+            if (kind, "pair", pair) not in live:
+                live[kind, "pair", pair] = work.tile(
+                    [P, 2, PAIR, 4], BF16, name=kind + "_grouped", bufs=bufs, align_bytes=64
+                )
+            grouped = live[kind, "pair", pair][:].rearrange("p g n f -> p (g n f)").bitcast(F32)
+            nc.scalar.copy(
+                out=grouped.rearrange("p (g n u) -> p g n u", g=2, u=2)[:, :, at : at + P, :],
+                in_=live[kind + " turned", t][:].rearrange("p g u n -> p g n u"),
+            )
+
+        def z_group(t):
+            if t >= LOWER:
+                group_pair("z", t, 2)
+                return
+            grouped = work.tile([P, 2 * HALF], BF16, name="z_grouped_one", align_bytes=64)
             nc.scalar.copy(
                 out=grouped[:].bitcast(F32).rearrange("p (g n u) -> p g n u", g=2, u=2),
-                in_=turned[:].rearrange("p g u n -> p g n u"),
+                in_=live["z turned", t][:].rearrange("p g u n -> p g n u"),
             )
-            live[tag, t] = grouped
+            live["z", "tile", t] = grouped
 
-        def quant(tag, t, codes_name):
-            codes = keep.tile([P, 2 * P], U32, name=codes_name + str(t), align_bytes=64)
-            scales = keep.tile([P, 2 * P], U8, name=codes_name + "s" + str(t), align_bytes=64)
-            nc.vector.quantize_mx(out=codes[:].bitcast(E4M3X4), scales=scales[:], in_=live[tag, t][:])
-            live[codes_name, t] = (codes, scales)
+        def quantise_tile(source, t, name):
+            codes = keep.tile([P, PAIR], U32, name=name + "_codes" + str(t), align_bytes=64)
+            scales = keep.tile([P, PAIR], U8, name=name + "_scales" + str(t), align_bytes=64)
+            nc.vector.quantize_mx(out=codes[:].bitcast(E4M3X4), scales=scales[:], in_=source[:])
+            live[name, t] = [(codes[:, g * P : (g + 1) * P], scales[:, g * P : (g + 1) * P]) for g in range(2)]
 
-        def product(codes_name, t, name, h, bank):
-            codes, scales = live[codes_name, t]
+        def upper_operands(codes, scales, t):
+            cols = slice((t - LOWER) * P, (t - LOWER + 1) * P)
+            return [(codes[:, g, cols], scales[:, g, cols]) for g in range(2)]
+
+        def z_quantise_pair(t, g):
+            cols = slice((t - LOWER) * P, (t - LOWER + 2) * P)
+            nc.vector.quantize_mx(
+                out=zq_upper[:, g, cols].bitcast(E4M3X4),
+                scales=zs_upper[:, g, cols],
+                in_=live["z", "pair", t // 2][:, g, :, :].rearrange("p n f -> p (n f)"),
+            )
+            for tile in (t, t + 1):
+                live["zq", tile] = upper_operands(zq_upper, zs_upper, tile)
+
+        def u1_group(out, b, t, moving):
+            at = b * 4 + t
             for g in range(2):
+                codes, scales = moving[g]
+                nc.tensor.matmul_mx(
+                    out=out,
+                    lhsT=a1_cols[:, g, at * PAIR : (at + 1) * PAIR].bitcast(E2M1X4),
+                    lhsT_scale=a1_plane[:, g, at * P : (at + 1) * P],
+                    rhs=codes.bitcast(E4M3X4),
+                    rhs_scale=scales,
+                    start=(g == 0),
+                    stop=(g == 1),
+                )
+
+        def u1_tile(tile, b):
+            bank = psum.tile([P, 4, P], F32, name="u1", tag="bank")
+            for t in range(4):
+                u1_group(bank[:, t, :], b, t, live["zq", tile])
+            live["u1", tile, b] = bank
+
+        def x1_tile(tile):
+            if ("x1", tile) not in live:
+                live["x1", tile] = work.tile([P, 2 * HALF], BF16, name="x1", align_bytes=64)
+            return live["x1", tile]
+
+        def gain(tile, b):
+            nc.vector.tensor_tensor(
+                out=x1_tile(tile)[:, b * HALF : (b + 1) * HALF].rearrange("p (n t) -> p n t", t=4),
+                in0=live["u1", tile, b][:].rearrange("p t n -> p n t"),
+                in1=g_cols[:, b : b + 1, :].to_broadcast([P, P, 4]),
+                op=ALU.mult,
+            )
+
+        def scale(tile, b):
+            scaled = work.tile([P, 4, P], BF16, name="x1_scaled", align_bytes=64)
+            for t in range(4):
+                nc.scalar.activation(
+                    out=scaled[:, t, :],
+                    in_=live["u1", tile, b][:, t, :],
+                    func=ACT.Copy,
+                    scale=g_cols[:, b, t : t + 1],
+                )
+            live["x1 scaled", tile, b] = scaled
+
+        def mix(tile, b):
+            nc.scalar.copy(
+                out=x1_tile(tile)[:, b * HALF : (b + 1) * HALF].rearrange("p (n t) -> p n t", t=4),
+                in_=live["x1 scaled", tile, b][:].rearrange("p t n -> p n t"),
+            )
+
+        def u1_wide(part):
+            b, first = part // 2, 2 * (part % 2)
+            if ("x1 wide", b) not in live:
+                live["x1 wide", b] = work.tile([P, 4, HALF], BF16, name="x1_wide", bufs=2, align_bytes=64)
+            for t in range(first, first + 2):
+                bank = psum.tile([P, HALF], F32, name="u1_wide", tag="bank")
+                u1_group(bank[:], b, t, [(zq_upper[:, g, :], zs_upper[:, g, :]) for g in range(2)])
+                nc.scalar.activation(
+                    out=live["x1 wide", b][:, t, :], in_=bank[:], func=ACT.Copy, scale=g_cols[:, b, t : t + 1]
+                )
+
+        def mix_wide(b, side):
+            cols = slice(side * PAIR, (side + 1) * PAIR)
+            if ("x1 mixed", b) not in live:
+                live["x1 mixed", b] = work.tile([P, HALF, 4], BF16, name="x1_mixed", bufs=2, align_bytes=64)
+            nc.scalar.copy(
+                out=live["x1 mixed", b][:, cols, :], in_=live["x1 wide", b][:, :, cols].rearrange("p t n -> p n t")
+            )
+
+        def x_quantise_wide(b):
+            nc.vector.quantize_mx(
+                out=xq_upper[:, b, :].bitcast(E4M3X4),
+                scales=xs_upper[:, b, :],
+                in_=live["x1 mixed", b][:].rearrange("p n t -> p (n t)"),
+            )
+            if b == 1:
+                for tile in range(LOWER, TILES):
+                    live["xq", tile] = upper_operands(xq_upper, xs_upper, tile)
+
+        def product(operand, name, t, h):
+            bank = psum.tile([P, HALF], F32, name="product", tag="bank")
+            for g in range(2):
+                codes, scales = live[operand, t][g]
                 nc.tensor.matmul_mx(
                     out=bank[:],
-                    lhsT=codes[:, g * P : (g + 1) * P].bitcast(E4M3X4),
-                    lhsT_scale=scales[:, g * P : (g + 1) * P],
+                    lhsT=codes.bitcast(E4M3X4),
+                    lhsT_scale=scales,
                     rhs=words[name][:, g, h * SIZE : (h + 1) * SIZE].bitcast(E2M1X4),
                     rhs_scale=planes[name][:, g, h * HALF : (h + 1) * HALF],
                     start=(g == 0),
                     stop=(g == 1),
                 )
+            return bank
 
-        def u1(t):
-            for h in range(2):
-                bank = psum.tile([P, HALF], F32, name="u1", tag="mm")
-                product("zq", t, "a1", h, bank)
-                live["u1", t, h] = bank
-
-        def u2(t):
-            for h in range(2):
-                bank = psum.tile([P, HALF], F32, name="u2", tag="u2", bufs=2)
-                product("zq", t, "a2", h, bank)
-                live["u2", t, h] = bank
+        def u2(t, h):
+            live["u2", t, h] = product("zq", "a2", t, h)
 
         def v(t, h):
-            bank = psum.tile([P, HALF], F32, name="v", tag="v", bufs=2)
-            product("xq", t, "s", h, bank)
-            live["v", t, h] = bank
-
-        def gain(t, h):
-            if h == 0:
-                x1 = work.tile([P, 2, HALF], BF16, name="x1", tag="x1", align_bytes=64)
-                live["x1", t] = x1
-            nc.vector.tensor_tensor(
-                out=live["x1", t][:, h, :].rearrange("p (u i e) -> p u i e", u=2, e=2),
-                in0=live["u1", t, h][:].rearrange("p (i u e) -> p u i e", u=2, e=2),
-                in1=g_bc[:, h * HALF : (h + 1) * HALF].rearrange("p (i u e) -> p u i e", u=2, e=2),
-                op=ALU.mult,
-            )
-
-        def turn(src, t, key):
-            turned = psum.tile([P, 2, 2, P], F32, name=key, tag="mm")
-            for g in range(2):
-                half_words = live[src, t][:, g, :].bitcast(F32)
-                for u in range(2):
-                    nc.tensor.transpose(turned[:, g, u, :], half_words[:, u * P : (u + 1) * P], ident[:])
-            live[key, t] = turned
+            live["v", t, h] = product("xq", "s", t, h)
 
         def add(t, h):
-            if h == 0:
-                live["vc", t] = work.tile([P, 2, HALF], F32, name="vc", tag="vc", align_bytes=64)
-                live["o", t] = work.tile([P, 2, HALF], F32, name="o", tag="o", align_bytes=64)
+            if ("v + c", t) not in live:
+                live["v + c", t] = work.tile([P, 2, HALF], F32, name="v_plus_c", bufs=8, align_bytes=64)
+                live["r", t] = work.tile([P, 2, HALF], F32, name="r", bufs=8, align_bytes=64)
             nc.vector.tensor_tensor(
-                out=live["vc", t][:, h, :], in0=live["v", t, h][:], in1=c_bc[:, h * HALF : (h + 1) * HALF], op=ALU.add
+                out=live["v + c", t][:, h, :],
+                in0=live["v", t, h][:],
+                in1=c_all[:, h * HALF : (h + 1) * HALF],
+                op=ALU.add,
             )
 
         def mul(t, h):
             nc.vector.tensor_tensor(
-                out=live["o", t][:, h, :], in0=live["u2", t, h][:], in1=live["vc", t][:, h, :], op=ALU.mult
+                out=live["r", t][:, h, :], in0=live["u2", t, h][:], in1=live["v + c", t][:, h, :], op=ALU.mult
             )
 
-        def store_rows(t, h):
-            rows = out_0[t * P : (t + 1) * P, :]
-            if h is None:
-                nc.sync.dma_start(out=rows, in_=live["o", t][:].rearrange("p h n -> p (h n)"))
-            else:
-                nc.sync.dma_start(out=rows[:, h * HALF : (h + 1) * HALF], in_=live["o", t][:, h, :])
+        def store_rows(t, halves):
+            nc.sync.dma_start(
+                out=out_0[t * P : (t + 1) * P, halves.start * HALF : halves.stop * HALF],
+                in_=live["r", t][:, halves, :].rearrange("p h n -> p (h n)"),
+            )
+
+        def rounded(t):
+            if ("r16", t) not in live:
+                live["r16", t] = work.tile([P, 2, HALF], BF16, name="r16", align_bytes=64)
+            return live["r16", t]
+
+        def by_word(ap):
+            return ap.rearrange("p (i u e) -> p u i e", u=2, e=2)
 
         def cast(t, h):
-            if h == 0:
-                live["ob", t] = work.tile([P, 2, HALF], BF16, name="ob", tag="ob", align_bytes=64)
             nc.scalar.copy(
-                out=live["ob", t][:, h, :].rearrange("p (u i e) -> p u i e", u=2, e=2),
-                in_=live["o", t][:, h, :].rearrange("p (i u e) -> p u i e", u=2, e=2),
+                out=rounded(t)[:, h, :].rearrange("p (u i e) -> p u i e", u=2, e=2), in_=by_word(live["r", t][:, h, :])
             )
 
-        def out_quant(t):
-            for g in range(2):
-                nc.vector.quantize_mx(
-                    out=oc[:, g, t * P : (t + 1) * P].bitcast(E4M3X4),
-                    scales=osc[:, g, t * P : (t + 1) * P],
-                    in_=live["oi", t][:, g * HALF : (g + 1) * HALF],
-                )
+        def last_cast(t, h):
+            nc.vector.tensor_tensor(
+                out=rounded(t)[:, h, :].rearrange("p (u i e) -> p u i e", u=2, e=2),
+                in0=by_word(live["u2", t, h][:]),
+                in1=by_word(live["v + c", t][:, h, :]),
+                op=ALU.mult,
+            )
 
-        def store_words(t0, t1):
+        def out_turn(t):
+            turned = psum.tile([P, 2, 2, P], F32, name="r_turned", tag="bank")
+            for h in range(2):
+                half_words = live["r16", t][:, h, :].bitcast(F32)
+                for u in range(2):
+                    nc.tensor.transpose(turned[:, h, u, :], half_words[:, u * P : (u + 1) * P], ident[:])
+            live["r turned", t] = turned
+
+        def out_turn_half(t, h):
+            turned = psum.tile([P, 2, P], F32, name="r_turned_half", tag="bank")
+            half_words = live["r16", t][:, h, :].bitcast(F32)
+            for u in range(2):
+                nc.tensor.transpose(turned[:, u, :], half_words[:, u * P : (u + 1) * P], ident[:])
+            live["r turned", t, h] = turned
+
+        def out_group_half(t, h):
+            at = (t % 2) * P
+            grouped = live["r", "pair", t // 2][:, h, at : at + P, :].rearrange("p n f -> p (n f)").bitcast(F32)
+            nc.scalar.copy(
+                out=grouped.rearrange("p (n u) -> p n u", u=2),
+                in_=live["r turned", t, h][:].rearrange("p u n -> p n u"),
+            )
+
+        def out_quantise(first, count, h):
+            n, inside, at = count * P, (first % 2) * P, (first % 4) * P
+            codes = oq_pair[first // 2] if count == 2 else oq_one[first % 2]
+            nc.vector.quantize_mx(
+                out=codes[:, h, :].bitcast(E4M3X4),
+                scales=os_half[first // LOWER][:, h, at : at + n],
+                in_=live["r", "pair", first // 2][:, h, inside : inside + n, :].rearrange("p n f -> p (n f)"),
+            )
+
+        def store_words(first, count):
+            codes = oq_pair[first // 2] if count == 2 else oq_one[first % 2]
             nc.sync.dma_start(
-                out=out_words[:, :, t0 * HALF : t1 * HALF].bitcast(I32), in_=oc[:, :, t0 * P : t1 * P].bitcast(I32)
+                out=out_words[:, :, first * HALF : (first + count) * HALF].bitcast(I32), in_=codes[:].bitcast(I32)
             )
 
-        def store_scales(t0, t1):
+        def store_scales(half):
             for q in range(4):
                 nc.sync.dma_start(
-                    out=out_2[:, 4 * q : 4 * q + 4, t0 * P : t1 * P].rearrange("g q m -> q g m").bitcast(I32),
-                    in_=osc[32 * q : 32 * q + 4, :, t0 * P : t1 * P].bitcast(I32),
+                    out=out_2[:, 4 * q : 4 * q + 4, half * HALF : (half + 1) * HALF]
+                    .rearrange("g q m -> q g m")
+                    .bitcast(I32),
+                    in_=os_half[half][32 * q : 32 * q + 4, :, :].bitcast(I32),
                 )
 
-        z_turn(0)
-        word_copy("zt", "zi", 0)
-        quant("zi", 0, "zq")
-        gc_turned = psum.tile([P, P], BF16, name="gct", tag="mm")
-        nc.tensor.transpose(gc_turned[:], gc_rows[:], ident_bf[:])
-        gc_cols = keep.tile([P, 16], BF16, name="gc_cols", align_bytes=64)
-        nc.vector.tensor_copy(out=gc_cols[:], in_=gc_turned[:, 0:16])
-        g_bc = keep.tile([P, SIZE], BF16, name="g_bc", align_bytes=64)
-        c_bc = keep.tile([P, SIZE], BF16, name="c_bc", align_bytes=64)
-
-        def spread(dst, first):
-            bank = psum.tile([P, SIZE], BF16, name="bc", tag="mm")
-            for m in range(8):
-                nc.tensor.transpose(
-                    bank[:, m * P : (m + 1) * P],
-                    gc_cols[:, first + m : first + m + 1].to_broadcast([P, P]),
-                    ident_bf[:],
-                )
-            nc.scalar.copy(out=dst[:], in_=bank[:])
-
-        spread(g_bc, 0)
-        u1(0)
-        gain(0, 0)
-        gain(0, 1)
-        z_turn(1)
-        word_copy("zt", "zi", 1)
-        quant("zi", 1, "zq")
-        spread(c_bc, 8)
-        turn("x1", 0, "xt")
-        z_turn(2)
-
-        for k in range(TILES):
-            word_copy("xt", "xi", k)
-            if k >= 2:
-                word_copy("ot", "oi", k - 2)
-            if k + 2 < TILES:
-                word_copy("zt", "zi", k + 2)
-            quant("xi", k, "xq")
-            if k + 1 < TILES:
-                u1(k + 1)
-            u2(k)
-            if k + 1 < TILES:
-                gain(k + 1, 0)
-            if k + 2 < TILES:
-                quant("zi", k + 2, "zq")
-            if k + 1 < TILES:
-                gain(k + 1, 1)
-            if k >= 2:
-                out_quant(k - 2)
-                if k % 2 == 1:
-                    store_words(k - 3, k - 1)
-                if k == 5:
-                    store_scales(0, 4)
-            v(k, 0)
-            v(k, 1)
-            if k >= 1:
-                cast(k - 1, 0)
-                cast(k - 1, 1)
-            last = k == TILES - 1
-            add(k, 0)
-            if last:
-                mul(k, 0)
-                store_rows(k, 0)
-                add(k, 1)
-            else:
-                add(k, 1)
-                mul(k, 0)
-            mul(k, 1)
-            store_rows(k, 1 if last else None)
-            if k + 1 < TILES:
-                turn("x1", k + 1, "xt")
-            if k >= 1:
-                turn("ob", k - 1, "ot")
-            if k + 3 < TILES:
-                z_turn(k + 3)
-
-        word_copy("ot", "oi", 6)
-        out_quant(6)
-        store_words(6, 7)
-        cast(7, 0)
-        cast(7, 1)
-        turn("ob", 7, "ot")
-        word_copy("ot", "oi", 7)
-        out_quant(7)
-        store_words(7, 8)
-        store_scales(4, 8)
+        stages = {
+            "biasturn": lambda i: bias_turn(),
+            "biasspread": lambda i: bias_spread(),
+            "gains": lambda i: gains(),
+            "perm": lambda i: permute(i // 2, i % 2),
+            "zorder": z_order,
+            "zturn": z_turn,
+            "zgroup": z_group,
+            "zquant": lambda t: quantise_tile(live["z", "tile", t], t, "zq"),
+            "zpairA": lambda t: z_quantise_pair(t, 0),
+            "zpairB": lambda t: z_quantise_pair(t, 1),
+            "u1A": lambda t: u1_tile(t, 0),
+            "u1B": lambda t: u1_tile(t, 1),
+            "gainA": lambda t: gain(t, 0),
+            "gainB": lambda t: gain(t, 1),
+            "scaleA": lambda t: scale(t, 0),
+            "scaleB": lambda t: scale(t, 1),
+            "mixA": lambda t: mix(t, 0),
+            "mixB": lambda t: mix(t, 1),
+            "xquant": lambda t: quantise_tile(live["x1", t], t, "xq"),
+            "u1wide": u1_wide,
+            "mixL": lambda b: mix_wide(b, 0),
+            "mixR": lambda b: mix_wide(b, 1),
+            "xwide": x_quantise_wide,
+            "u2A": lambda t: u2(t, 0),
+            "u2B": lambda t: u2(t, 1),
+            "vA": lambda t: v(t, 0),
+            "vB": lambda t: v(t, 1),
+            "addA": lambda t: add(t, 0),
+            "addB": lambda t: add(t, 1),
+            "mulA": lambda t: mul(t, 0),
+            "mulB": lambda t: mul(t, 1),
+            "lastA": lambda t: last_cast(t, 0),
+            "lastB": lambda t: last_cast(t, 1),
+            "rows": lambda t: store_rows(t, slice(0, 2)),
+            "rowsA": lambda t: store_rows(t, slice(0, 1)),
+            "rowsB": lambda t: store_rows(t, slice(1, 2)),
+            "castA": lambda t: cast(t, 0),
+            "castB": lambda t: cast(t, 1),
+            "oturn": out_turn,
+            "oturnA": lambda t: out_turn_half(t, 0),
+            "oturnB": lambda t: out_turn_half(t, 1),
+            "ogroup": lambda t: group_pair("r", t, 4),
+            "ogroupA": lambda t: out_group_half(t, 0),
+            "ogroupB": lambda t: out_group_half(t, 1),
+            "opairA": lambda t: out_quantise(t, 2, 0),
+            "opairB": lambda t: out_quantise(t, 2, 1),
+            "ooneA": lambda t: out_quantise(t, 1, 0),
+            "ooneB": lambda t: out_quantise(t, 1, 1),
+            "wordpair": lambda t: store_words(t, 2),
+            "wordone": lambda t: store_words(t, 1),
+            "scales": store_scales,
+        }
+        for row in ORDER:
+            for entry in row.split():
+                stages[entry[:-1]](int(entry[-1]))

from contextlib import ExitStack

import concourse.mybir as mybir

F32 = mybir.dt.float32
BF16 = mybir.dt.bfloat16
I32 = mybir.dt.int32
U32 = mybir.dt.uint32
U8 = mybir.dt.uint8
E4M3X4 = mybir.dt.float8_e4m3fn_x4
E2M1X4 = mybir.dt.float4_e2m1fn_x4
ALU = mybir.AluOpType
ACT = mybir.ActivationFunctionType

P = 128
SIZE = 1024
HALF = 512
PAIR = 2 * P
TILES = SIZE // P
LOWER = 4
FLOPS = 3 * 2 * SIZE * SIZE * SIZE

ORDER = (
    "perm0 zturn0 biasturn0 zgroup0 zturn1 perm1 zgroup1 biasspread0 perm2 zquant0 perm3 zturn2 gains0",
    "u1A0 zquant1 zgroup2 gainA0 zorder3 u1B0 zorder4 u1A1 u1B1 gainB0 zorder5",
    "zturn3 zorder6 gainA1 zturn4 zturn5 xquant0 zturn6 zquant2 zorder7 zgroup3 zquant3 zturn7 gainB1",
    "u1A2 u1B2 gainA2 zgroup4 u1A3 zgroup5 zpairA4 zpairB4 zgroup6 u1B3 zgroup7 zpairA6 zpairB6 gainB2",
    "scaleA3 xquant1",
    "vA0 xquant2 u2A0 scaleB3 mixA3 u1wide0 u1wide1 addA0 vB0 mulA0 addB0 vA1 mixL0 u2B0 mixR0 vB1 addA1",
    "mixB3",
    "u2A1 u1wide2 vA2 addB1 u1wide3 mulB0 rows0 u2B1 mixR1 mixL1 mulA1 u2A2 vB2 addA2 xwide0 castA0",
    "xquant3 mulB1 rows1",
    "vA3 mulA2 addB2 castB0 addA3 u2B2 mulB2 rows2 vB3 castA1 u2A3 u2B3 addB3 u2A4 xwide1",
    "vA4 vB4 oturn0 castB1 oturn1 mulA3 mulB3 rows3 castA2 castB2",
    "vA5 addA4 u2B4 castA3 u2A5 ogroup0 addB4 mulA4 castB3 vB5 addA5 ogroup1 u2B5 mulB4 rows4 castA4",
    "mulA5",
    "vA6 addB5 oturn2 opairB0 opairA0 wordpair0 addA6 mulB5 rows5 vB6 ogroup2 castB4",
    "vA7 u2A6 oturn3 vB7 u2B6 castA5 oturn4 castB5 ogroup3 u2A7 addB6 u2B7 addA7 mulA6 addB7 mulB6 rows6",
    "castA6 ogroup4 castB6 opairA2 opairB2 scales0 wordpair2 oturn5 mulA7 rowsA7 lastA7 oturn6 ogroup5",
    "lastB7 opairB4 opairA4 wordpair4",
    "oturnA7 ogroup6 ooneA6 ogroupA7 oturnB7 ooneB6 wordone6 ooneA7 ogroupB7 ooneB7 wordone7 scales1",
    "mulB7 rowsB7",
)


def tile_pinetnestedcoupledcpdegreetwo_x2_kernel(
    tc, z, a1_words, a1_scales, g1, s_words, s_scales, c, a2_words, a2_scales, out_0, out_1, out_2
):
    nc = tc.nc
    out_words = out_1.rearrange("g p m b -> p g (m b)")

    with ExitStack() as ctx:
        keep = ctx.enter_context(tc.tile_pool(name="keep", bufs=1))
        work = ctx.enter_context(tc.tile_pool(name="work", bufs=5))
        psum = ctx.enter_context(tc.psum_pool(name="psum", bufs=8))
        ctx.enter_context(tc.manual_schedule())
        live = {}

        c_rows = keep.tile([P, P], BF16, name="c_rows", align_bytes=64)
        nc.vector.memset(c_rows[:], 0.0)
        words = {}
        planes = {}
        for name in ("a2", "s"):
            words[name] = keep.tile([P, 2, 2 * SIZE], U8, name=name + "_words_sb", align_bytes=64)
        for name in ("a1", "a2", "s"):
            planes[name] = keep.tile([P, 2, SIZE], U8, name=name + "_plane", align_bytes=64)

        def clear(name):
            nc.vector.memset(planes[name][:].rearrange("p g n -> p (g n)").bitcast(I32), 0)

        clear("a1")
        diff = keep.tile([P, P], I32, name="diff", align_bytes=64)
        nc.gpsimd.iota(diff[:], pattern=[[-1, P]], base=0, channel_multiplier=1)
        ident = keep.tile([P, P], F32, name="ident", align_bytes=64)
        ident_bf = keep.tile([P, P], BF16, name="ident_bf", align_bytes=64)
        nc.vector.tensor_single_scalar(out=ident[:], in_=diff[:], scalar=0, op=ALU.is_equal)
        nc.vector.tensor_single_scalar(out=ident_bf[:], in_=diff[:], scalar=0, op=ALU.is_equal)
        clear("a2")
        clear("s")

        z_sb = [keep.tile([P, SIZE], BF16, name="z_sb" + str(t), align_bytes=64) for t in range(TILES)]
        a1_raw = [keep.tile([P, 2, SIZE], U8, name="a1_raw" + str(b), align_bytes=64) for b in range(2)]
        a1_cols = keep.tile([P, 2, 2 * SIZE], U8, name="a1_cols", align_bytes=64)
        a1_plane = keep.tile([P, 2, SIZE], U8, name="a1_plane_cols", align_bytes=64)
        g_raw = keep.tile([P, 2, 4], BF16, name="g_raw", align_bytes=64)
        g_cols = keep.tile([P, 2, 4], F32, name="g_cols", align_bytes=64)
        c_cols = keep.tile([P, 8], BF16, name="c_cols", align_bytes=64)
        c_all = keep.tile([P, SIZE], BF16, name="c_all", align_bytes=64)
        zq_upper = keep.tile([P, 2, HALF], U32, name="zq_upper", align_bytes=64)
        zs_upper = keep.tile([P, 2, HALF], U8, name="zs_upper", align_bytes=64)
        xq_upper = keep.tile([P, 2, HALF], U32, name="xq_upper", align_bytes=64)
        xs_upper = keep.tile([P, 2, HALF], U8, name="xs_upper", align_bytes=64)
        oq_pair = [keep.tile([P, 2, PAIR], U32, name="oq_pair" + str(i), align_bytes=64) for i in range(3)]
        oq_one = [keep.tile([P, 2, P], U32, name="oq_one" + str(i), align_bytes=64) for i in range(2)]
        os_half = [keep.tile([P, 2, HALF], U8, name="os_half" + str(i), align_bytes=64) for i in range(2)]

        def load_z(t):
            nc.sync.dma_start(out=z_sb[t][:], in_=z[t * P : (t + 1) * P, :])

        def load_a1(b):
            nc.sync.dma_start(
                out=a1_raw[b][:].bitcast(I32),
                in_=a1_words.rearrange("g p b -> p g b")[:, :, b * SIZE : (b + 1) * SIZE].bitcast(I32),
            )

        def load_words(name, src):
            nc.sync.dma_start(out=words[name][:].bitcast(I32), in_=src.rearrange("g p b -> p g b").bitcast(I32))

        def load_scales(name, src, queue):
            for q in range(4):
                queue.dma_start(
                    out=planes[name][32 * q : 32 * q + 4, :, :].bitcast(I32),
                    in_=src[:, 4 * q : 4 * q + 4, :].rearrange("g q n -> q g n").bitcast(I32),
                )

        load_a1(0)
        load_scales("a1", a1_scales, nc.scalar)
        load_z(0)
        load_a1(1)
        nc.gpsimd.dma_start(out=c_rows[0:8, :], in_=c.rearrange("(r n) -> r n", n=P))
        nc.gpsimd.dma_start(out=g_raw[:], in_=g1.rearrange("(g p t) -> p g t", p=P, t=4))
        load_z(1)
        load_scales("s", s_scales, nc.sync)
        load_words("s", s_words)
        load_z(2)
        load_scales("a2", a2_scales, nc.sync)
        load_words("a2", a2_words)
        for t in range(3, TILES):
            load_z(t)

        def bias_turn():
            turned = psum.tile([P, P], BF16, name="c_turned", tag="bank")
            nc.tensor.transpose(turned[:], c_rows[:], ident_bf[:])
            nc.scalar.copy(out=c_cols[:], in_=turned[:, 0:8])

        def bias_spread():
            bank = psum.tile([P, SIZE], BF16, name="c_spread", tag="bank")
            for m in range(8):
                nc.tensor.transpose(
                    bank[:, m * P : (m + 1) * P], c_cols[:, m : m + 1].to_broadcast([P, P]), ident_bf[:]
                )
            nc.scalar.copy(out=c_all[:], in_=bank[:])

        def gains():
            nc.vector.tensor_copy(
                out=g_cols[:].rearrange("p g t -> p (g t)"), in_=g_raw[:].rearrange("p g t -> p (g t)")
            )

        def permute(b, g):
            nc.vector.tensor_copy(
                out=a1_cols[:, g, b * SIZE : (b + 1) * SIZE].rearrange("p (t m c) -> p t m c", t=4, c=2),
                in_=a1_raw[b][:, g, :].rearrange("p (m t c) -> p t m c", t=4, c=2),
            )
            nc.vector.tensor_copy(
                out=a1_plane[:, g, b * HALF : (b + 1) * HALF].rearrange("p (t m) -> p t m", t=4),
                in_=planes["a1"][:, g, b * HALF : (b + 1) * HALF].rearrange("p (m t) -> p t m", t=4),
            )

        def z_order(t):
            ordered = work.tile([P, 2, 2, P], F32, name="z_words", tag="z_words", align_bytes=64)
            nc.scalar.copy(
                out=ordered[:], in_=z_sb[t][:].bitcast(F32).rearrange("p (g w u) -> p g u w", g=2, u=2)
            )
            live["z words", t] = ordered

        def z_turn(t):
            turned = psum.tile([P, 2, 2, P], F32, name="z_turned", tag="bank")
            for g in range(2):
                for u in range(2):
                    if t < 3:
                        source = z_sb[t][:].bitcast(F32)[:, 256 * g + u : 256 * (g + 1) : 2]
                    else:
                        source = live["z words", t][:, g, u, :]
                    nc.tensor.transpose(turned[:, g, u, :], source, ident[:])
            live["z turned", t] = turned

        def group_pair(kind, t, bufs):
            pair, at = t // 2, (t % 2) * P
            if (kind, "pair", pair) not in live:
                live[kind, "pair", pair] = work.tile(
                    [P, 2, PAIR, 4], BF16, name=kind + "_grouped", bufs=bufs, align_bytes=64
                )
            grouped = live[kind, "pair", pair][:].rearrange("p g n f -> p (g n f)").bitcast(F32)
            nc.scalar.copy(
                out=grouped.rearrange("p (g n u) -> p g n u", g=2, u=2)[:, :, at : at + P, :],
                in_=live[kind + " turned", t][:].rearrange("p g u n -> p g n u"),
            )

        def z_group(t):
            if t >= LOWER:
                group_pair("z", t, 2)
                return
            grouped = work.tile([P, 2 * HALF], BF16, name="z_grouped_one", align_bytes=64)
            nc.scalar.copy(
                out=grouped[:].bitcast(F32).rearrange("p (g n u) -> p g n u", g=2, u=2),
                in_=live["z turned", t][:].rearrange("p g u n -> p g n u"),
            )
            live["z", "tile", t] = grouped

        def quantise_tile(source, t, name):
            codes = keep.tile([P, PAIR], U32, name=name + "_codes" + str(t), align_bytes=64)
            scales = keep.tile([P, PAIR], U8, name=name + "_scales" + str(t), align_bytes=64)
            nc.vector.quantize_mx(out=codes[:].bitcast(E4M3X4), scales=scales[:], in_=source[:])
            live[name, t] = [(codes[:, g * P : (g + 1) * P], scales[:, g * P : (g + 1) * P]) for g in range(2)]

        def upper_operands(codes, scales, t):
            cols = slice((t - LOWER) * P, (t - LOWER + 1) * P)
            return [(codes[:, g, cols], scales[:, g, cols]) for g in range(2)]

        def z_quantise_pair(t, g):
            cols = slice((t - LOWER) * P, (t - LOWER + 2) * P)
            nc.vector.quantize_mx(
                out=zq_upper[:, g, cols].bitcast(E4M3X4),
                scales=zs_upper[:, g, cols],
                in_=live["z", "pair", t // 2][:, g, :, :].rearrange("p n f -> p (n f)"),
            )
            for tile in (t, t + 1):
                live["zq", tile] = upper_operands(zq_upper, zs_upper, tile)

        def u1_group(out, b, t, moving):
            at = b * 4 + t
            for g in range(2):
                codes, scales = moving[g]
                nc.tensor.matmul_mx(
                    out=out,
                    lhsT=a1_cols[:, g, at * PAIR : (at + 1) * PAIR].bitcast(E2M1X4),
                    lhsT_scale=a1_plane[:, g, at * P : (at + 1) * P],
                    rhs=codes.bitcast(E4M3X4),
                    rhs_scale=scales,
                    start=(g == 0),
                    stop=(g == 1),
                )

        def u1_tile(tile, b):
            bank = psum.tile([P, 4, P], F32, name="u1", tag="bank")
            for t in range(4):
                u1_group(bank[:, t, :], b, t, live["zq", tile])
            live["u1", tile, b] = bank

        def x1_tile(tile):
            if ("x1", tile) not in live:
                live["x1", tile] = work.tile([P, 2 * HALF], BF16, name="x1", align_bytes=64)
            return live["x1", tile]

        def gain(tile, b):
            nc.vector.tensor_tensor(
                out=x1_tile(tile)[:, b * HALF : (b + 1) * HALF].rearrange("p (n t) -> p n t", t=4),
                in0=live["u1", tile, b][:].rearrange("p t n -> p n t"),
                in1=g_cols[:, b : b + 1, :].to_broadcast([P, P, 4]),
                op=ALU.mult,
            )

        def scale(tile, b):
            scaled = work.tile([P, 4, P], BF16, name="x1_scaled", align_bytes=64)
            for t in range(4):
                nc.scalar.activation(
                    out=scaled[:, t, :],
                    in_=live["u1", tile, b][:, t, :],
                    func=ACT.Copy,
                    scale=g_cols[:, b, t : t + 1],
                )
            live["x1 scaled", tile, b] = scaled

        def mix(tile, b):
            nc.scalar.copy(
                out=x1_tile(tile)[:, b * HALF : (b + 1) * HALF].rearrange("p (n t) -> p n t", t=4),
                in_=live["x1 scaled", tile, b][:].rearrange("p t n -> p n t"),
            )

        def u1_wide(part):
            b, first = part // 2, 2 * (part % 2)
            if ("x1 wide", b) not in live:
                live["x1 wide", b] = work.tile([P, 4, HALF], BF16, name="x1_wide", bufs=2, align_bytes=64)
            for t in range(first, first + 2):
                bank = psum.tile([P, HALF], F32, name="u1_wide", tag="bank")
                u1_group(bank[:], b, t, [(zq_upper[:, g, :], zs_upper[:, g, :]) for g in range(2)])
                nc.scalar.activation(
                    out=live["x1 wide", b][:, t, :], in_=bank[:], func=ACT.Copy, scale=g_cols[:, b, t : t + 1]
                )

        def mix_wide(b, side):
            cols = slice(side * PAIR, (side + 1) * PAIR)
            if ("x1 mixed", b) not in live:
                live["x1 mixed", b] = work.tile([P, HALF, 4], BF16, name="x1_mixed", bufs=2, align_bytes=64)
            nc.scalar.copy(
                out=live["x1 mixed", b][:, cols, :], in_=live["x1 wide", b][:, :, cols].rearrange("p t n -> p n t")
            )

        def x_quantise_wide(b):
            nc.vector.quantize_mx(
                out=xq_upper[:, b, :].bitcast(E4M3X4),
                scales=xs_upper[:, b, :],
                in_=live["x1 mixed", b][:].rearrange("p n t -> p (n t)"),
            )
            if b == 1:
                for tile in range(LOWER, TILES):
                    live["xq", tile] = upper_operands(xq_upper, xs_upper, tile)

        def product(operand, name, t, h):
            bank = psum.tile([P, HALF], F32, name="product", tag="bank")
            for g in range(2):
                codes, scales = live[operand, t][g]
                nc.tensor.matmul_mx(
                    out=bank[:],
                    lhsT=codes.bitcast(E4M3X4),
                    lhsT_scale=scales,
                    rhs=words[name][:, g, h * SIZE : (h + 1) * SIZE].bitcast(E2M1X4),
                    rhs_scale=planes[name][:, g, h * HALF : (h + 1) * HALF],
                    start=(g == 0),
                    stop=(g == 1),
                )
            return bank

        def u2(t, h):
            live["u2", t, h] = product("zq", "a2", t, h)

        def v(t, h):
            live["v", t, h] = product("xq", "s", t, h)

        def add(t, h):
            if ("v + c", t) not in live:
                live["v + c", t] = work.tile([P, 2, HALF], F32, name="v_plus_c", bufs=8, align_bytes=64)
                live["r", t] = work.tile([P, 2, HALF], F32, name="r", bufs=8, align_bytes=64)
            nc.vector.tensor_tensor(
                out=live["v + c", t][:, h, :],
                in0=live["v", t, h][:],
                in1=c_all[:, h * HALF : (h + 1) * HALF],
                op=ALU.add,
            )

        def mul(t, h):
            nc.vector.tensor_tensor(
                out=live["r", t][:, h, :], in0=live["u2", t, h][:], in1=live["v + c", t][:, h, :], op=ALU.mult
            )

        def store_rows(t, halves):
            nc.sync.dma_start(
                out=out_0[t * P : (t + 1) * P, halves.start * HALF : halves.stop * HALF],
                in_=live["r", t][:, halves, :].rearrange("p h n -> p (h n)"),
            )

        def rounded(t):
            if ("r16", t) not in live:
                live["r16", t] = work.tile([P, 2, HALF], BF16, name="r16", align_bytes=64)
            return live["r16", t]

        def by_word(ap):
            return ap.rearrange("p (i u e) -> p u i e", u=2, e=2)

        def cast(t, h):
            nc.scalar.copy(
                out=rounded(t)[:, h, :].rearrange("p (u i e) -> p u i e", u=2, e=2), in_=by_word(live["r", t][:, h, :])
            )

        def last_cast(t, h):
            nc.vector.tensor_tensor(
                out=rounded(t)[:, h, :].rearrange("p (u i e) -> p u i e", u=2, e=2),
                in0=by_word(live["u2", t, h][:]),
                in1=by_word(live["v + c", t][:, h, :]),
                op=ALU.mult,
            )

        def out_turn(t):
            turned = psum.tile([P, 2, 2, P], F32, name="r_turned", tag="bank")
            for h in range(2):
                half_words = live["r16", t][:, h, :].bitcast(F32)
                for u in range(2):
                    nc.tensor.transpose(turned[:, h, u, :], half_words[:, u * P : (u + 1) * P], ident[:])
            live["r turned", t] = turned

        def out_turn_half(t, h):
            turned = psum.tile([P, 2, P], F32, name="r_turned_half", tag="bank")
            half_words = live["r16", t][:, h, :].bitcast(F32)
            for u in range(2):
                nc.tensor.transpose(turned[:, u, :], half_words[:, u * P : (u + 1) * P], ident[:])
            live["r turned", t, h] = turned

        def out_group_half(t, h):
            at = (t % 2) * P
            grouped = live["r", "pair", t // 2][:, h, at : at + P, :].rearrange("p n f -> p (n f)").bitcast(F32)
            nc.scalar.copy(
                out=grouped.rearrange("p (n u) -> p n u", u=2),
                in_=live["r turned", t, h][:].rearrange("p u n -> p n u"),
            )

        def out_quantise(first, count, h):
            n, inside, at = count * P, (first % 2) * P, (first % 4) * P
            codes = oq_pair[first // 2] if count == 2 else oq_one[first % 2]
            nc.vector.quantize_mx(
                out=codes[:, h, :].bitcast(E4M3X4),
                scales=os_half[first // LOWER][:, h, at : at + n],
                in_=live["r", "pair", first // 2][:, h, inside : inside + n, :].rearrange("p n f -> p (n f)"),
            )

        def store_words(first, count):
            codes = oq_pair[first // 2] if count == 2 else oq_one[first % 2]
            nc.sync.dma_start(
                out=out_words[:, :, first * HALF : (first + count) * HALF].bitcast(I32), in_=codes[:].bitcast(I32)
            )

        def store_scales(half):
            for q in range(4):
                nc.sync.dma_start(
                    out=out_2[:, 4 * q : 4 * q + 4, half * HALF : (half + 1) * HALF]
                    .rearrange("g q m -> q g m")
                    .bitcast(I32),
                    in_=os_half[half][32 * q : 32 * q + 4, :, :].bitcast(I32),
                )

        stages = {
            "biasturn": lambda i: bias_turn(),
            "biasspread": lambda i: bias_spread(),
            "gains": lambda i: gains(),
            "perm": lambda i: permute(i // 2, i % 2),
            "zorder": z_order,
            "zturn": z_turn,
            "zgroup": z_group,
            "zquant": lambda t: quantise_tile(live["z", "tile", t], t, "zq"),
            "zpairA": lambda t: z_quantise_pair(t, 0),
            "zpairB": lambda t: z_quantise_pair(t, 1),
            "u1A": lambda t: u1_tile(t, 0),
            "u1B": lambda t: u1_tile(t, 1),
            "gainA": lambda t: gain(t, 0),
            "gainB": lambda t: gain(t, 1),
            "scaleA": lambda t: scale(t, 0),
            "scaleB": lambda t: scale(t, 1),
            "mixA": lambda t: mix(t, 0),
            "mixB": lambda t: mix(t, 1),
            "xquant": lambda t: quantise_tile(live["x1", t], t, "xq"),
            "u1wide": u1_wide,
            "mixL": lambda b: mix_wide(b, 0),
            "mixR": lambda b: mix_wide(b, 1),
            "xwide": x_quantise_wide,
            "u2A": lambda t: u2(t, 0),
            "u2B": lambda t: u2(t, 1),
            "vA": lambda t: v(t, 0),
            "vB": lambda t: v(t, 1),
            "addA": lambda t: add(t, 0),
            "addB": lambda t: add(t, 1),
            "mulA": lambda t: mul(t, 0),
            "mulB": lambda t: mul(t, 1),
            "lastA": lambda t: last_cast(t, 0),
            "lastB": lambda t: last_cast(t, 1),
            "rows": lambda t: store_rows(t, slice(0, 2)),
            "rowsA": lambda t: store_rows(t, slice(0, 1)),
            "rowsB": lambda t: store_rows(t, slice(1, 2)),
            "castA": lambda t: cast(t, 0),
            "castB": lambda t: cast(t, 1),
            "oturn": out_turn,
            "oturnA": lambda t: out_turn_half(t, 0),
            "oturnB": lambda t: out_turn_half(t, 1),
            "ogroup": lambda t: group_pair("r", t, 4),
            "ogroupA": lambda t: out_group_half(t, 0),
            "ogroupB": lambda t: out_group_half(t, 1),
            "opairA": lambda t: out_quantise(t, 2, 0),
            "opairB": lambda t: out_quantise(t, 2, 1),
            "ooneA": lambda t: out_quantise(t, 1, 0),
            "ooneB": lambda t: out_quantise(t, 1, 1),
            "wordpair": lambda t: store_words(t, 2),
            "wordone": lambda t: store_words(t, 1),
            "scales": store_scales,
        }
        for row in ORDER:
            for entry in row.split():
                stages[entry[:-1]](int(entry[-1]))
